import numpy as np
import ml_dtypes


def mxq(x, axis, fmt="e4m3"):
    dtype, down = {"e4m3": (ml_dtypes.float8_e4m3fn, 7), "e5m2": (ml_dtypes.float8_e5m2, 14)}[fmt]
    v = np.moveaxis(np.asarray(x, np.float32).astype(ml_dtypes.bfloat16).astype(np.float64), axis, -1)
    blocks = v.reshape(v.shape[:-1] + (-1, 32))
    amax = np.abs(blocks).max(-1, keepdims=True)
    byte = np.maximum(np.where(amax > 0, np.frexp(amax)[1] - 1 + 127, 0) - down, 1)
    scale = np.exp2(byte - 127.0)
    codes = (blocks / scale).astype(np.float32).astype(dtype).astype(np.float64)
    return np.moveaxis((codes * scale).reshape(v.shape), -1, axis)


WIDE = False


def mx_kscale(k):
    if not WIDE:
        return np.ones(k)
    levels = np.array([10, -10, 5, -5, 0])
    if k % 512:
        return np.exp2(np.random.permutation(np.resize(levels, k // 32))).repeat(32)
    a = np.empty((k // 512, 16))
    for p in range(k // 512):
        a[p, :8] = np.random.permutation(np.resize(levels, 8))
        for g in range(8):
            far = levels[np.abs(levels - a[p, g]) >= 10]
            a[p, g + 8] = far[np.random.randint(len(far))]
    return np.exp2(a.ravel()).repeat(32)


def f64(x):
    return np.asarray(x).astype(np.float64)


def striped(idx):
    return np.tile(idx.reshape(-1, 16).T, (8, 1)).astype(np.uint16)


def unstriped(offs):
    return offs[:16].T.reshape(-1).astype(np.int64)


E2M1 = np.array([0.0, 0.5, 1.0, 1.5, 2.0, 3.0, 4.0, 6.0, -0.0, -0.5, -1.0, -1.5, -2.0, -3.0, -4.0, -6.0])


def pack_weight(w, fmt):
    k, n = w.shape
    w = f64(np.asarray(w, np.float32).astype(ml_dtypes.bfloat16)).reshape(k // 32, 32, n)
    amax = np.abs(w).max(1)
    if fmt == "e4m3":
        byte = np.frexp(amax)[1] - 1 + 127 - 7
    else:
        mant, ex = np.frexp(amax / 6.0)
        byte = np.where(mant > 0.5, ex, ex - 1) + 127
    byte = np.clip(np.where(amax > 0, byte, 1), 1, 254)
    scaled = (w * np.exp2(127.0 - byte)[:, None, :]).reshape(k, n).astype(np.float32)
    by_word = np.ascontiguousarray(scaled.reshape(k // 512, 128, 4, n).transpose(0, 1, 3, 2))
    if fmt == "e4m3":
        words = by_word.astype(ml_dtypes.float8_e4m3fn).view(np.uint8)
    else:
        c = by_word.astype(ml_dtypes.float4_e2m1fn).view(np.uint8) & 0xF
        words = (c[..., 0::2] | (c[..., 1::2] << 4)).reshape(k // 512, 128, 2 * n)
    return np.ascontiguousarray(words), np.ascontiguousarray(byte.astype(np.uint8).reshape(k // 512, 16, n))


def unpack_weight(words, scales, fmt):
    g, _, n = scales.shape
    words = np.ascontiguousarray(words).reshape(g, 128, n, -1)
    if fmt == "e4m3":
        vals = words.view(ml_dtypes.float8_e4m3fn).astype(np.float64)
    else:
        nib = np.empty((g, 128, n, 4), np.uint8)
        nib[..., 0::2] = words & 0xF
        nib[..., 1::2] = words >> 4
        vals = E2M1[nib]
    vals = vals * np.repeat(np.exp2(scales.astype(np.float64) - 127.0), 8, axis=1)[..., None]
    return vals.transpose(0, 1, 3, 2).reshape(g * 512, n)


def gelu(v):
    return 0.5 * v * (1.0 + np.tanh(np.sqrt(2.0 / np.pi) * (v + 0.044715 * v**3)))


def striped8(idx):
    return np.concatenate([v.reshape(-1, 16).T for v in idx]).astype(np.uint16)


def unstriped8(offs):
    return np.stack([offs[16 * g:16 * g + 16].T.reshape(-1) for g in range(8)]).astype(np.int64)


def heads(h, wgt, idx8):
    r = np.arange(h.shape[0])
    return wgt[r // 4 % 128] * h[r[:, None], idx8[r % 512 // 64]]


def put_heads(h, wgs, idx8, t2):
    r = np.arange(h.shape[0])
    page = np.zeros((h.shape[0], t2))
    page[r[:, None], idx8[r % 512 // 64]] = wgs[r // 4 % 128] * h
    return page


K, T, S, H, N, P, T2 = 512, 4096, 1024, 1024, 1024, 512, 1024

def setup_inputs():
    n = np.random.standard_normal
    s = mx_kscale(K)[:, None]
    u = mx_kscale(H)[:, None]
    d = {}
    d["tab_words"], d["tab_scales"] = pack_weight(n((K, T)) * s, "e4m3")
    d["offs"] = striped(np.random.permutation(T)[:S])
    d["w1"] = (3.0 * n((K, H)) / s / K ** 0.5).astype(np.float32)
    d["w2_words"], d["w2_scales"] = pack_weight(n((K, H)) / s * u.T / K ** 0.5, "e2m1")
    d["gain"] = (1.4 * np.exp(0.3 * n(H)) * u[:, 0]).astype(np.float32)
    d["offs2"] = striped8(np.stack([np.random.permutation(S)[:P] for _ in range(8)]))
    d["wgt"] = np.repeat(np.random.uniform(0.5, 2.0, (8, P)), 16, axis=0).astype(np.float32)
    d["vec"] = np.exp(0.4 * n(H)).astype(np.float32)
    d["w3"] = (0.5 * n((H, N)) / u / H ** 0.5).astype(np.float32)
    d["w4_words"], d["w4_scales"] = pack_weight(0.5 * n((H, N)) / u / H ** 0.5, "e4m3")
    d["offs3"] = striped8(np.stack([np.random.permutation(T2)[:P] for _ in range(8)]))
    d["wgo"] = np.repeat(np.random.uniform(0.5, 2.0, (8, P)), 16, axis=0).astype(np.float32)
    return d

def reference(tab_words, tab_scales, offs, w1, w2_words, w2_scales, gain, offs2, wgt, vec, w3, w4_words, w4_scales, offs3, wgo):
    v = unpack_weight(tab_words, tab_scales, "e4m3")[:, unstriped(offs)]
    a = mxq(f64(w1), 0, "e4m3").T @ v
    b = unpack_weight(w2_words, w2_scales, "e2m1").T @ v
    h = f64(gain)[:, None] * np.log(1.0 + np.abs(a)) + b
    x = heads(h, f64(wgt), unstriped8(offs2))
    z = mxq(f64(vec)[:, None] * x, 0, "e4m3")
    y1 = mxq(f64(w3), 0, "e4m3").T @ z
    y2 = unpack_weight(w4_words, w4_scales, "e4m3").T @ z
    y = np.maximum(np.abs(y1), np.abs(y2))
    return put_heads(y, f64(wgo), unstriped8(offs3), T2)

@@ -1,0 +1,271 @@
+from contextlib import ExitStack
+
+import concourse.mybir as mybir
+
+K, T, S, H, N, M, T2 = 512, 4096, 1024, 1024, 1024, 512, 1024
+FLOPS = 2 * (2 * K * H * S + 2 * H * N * M)
+
+F32 = mybir.dt.float32
+BF16 = mybir.dt.bfloat16
+I32 = mybir.dt.int32
+U32 = mybir.dt.uint32
+U16 = mybir.dt.uint16
+U8 = mybir.dt.uint8
+FP8X4 = mybir.dt.float8_e4m3fn_x4
+FP4X4 = mybir.dt.float4_e2m1fn_x4
+ALU = mybir.AluOpType
+ACT = mybir.ActivationFunctionType
+
+P = 128
+BANK = 512
+PAGES = 3
+
+
+def tile_list_inflator_severity_filing_kernel(
+    tc, tab_words, tab_scales, offs, w1, w2_words, w2_scales, gain, offs2, wgt, vec, w3, w4_words, w4_scales, offs3, wgo, out
+):
+    nc = tc.nc
+    with ExitStack() as ctx:
+        keep = ctx.enter_context(tc.tile_pool(name="keep", bufs=1))
+        ring = ctx.enter_context(tc.tile_pool(name="ring", bufs=2))
+        psum = ctx.enter_context(tc.psum_pool(name="psum", bufs=1))
+
+        def kept(shape, dtype, name):
+            return keep.tile(shape, dtype, name=name, align_bytes=64)
+
+        def shared(shape, dtype, name, tag):
+            return keep.tile(shape, dtype, name=name, tag=tag, align_bytes=64)
+
+        list1 = kept([P, S // 16], U16, "list1")
+        list2 = kept([P, M // 16], U16, "list2")
+        list3 = kept([P, M // 16], U16, "list3")
+        tab_s = shared([P, T], U8, "tab_s", "slot_c")
+        s2_raw = shared([P, H], U8, "s2_raw", "slot_e")
+        s2 = kept([P, H], U8, "s2")
+        s4 = kept([P, H], U8, "s4")
+        warm = shared([P, 2], F32, "warm", "slot_a")
+        w2_raw = shared([P, 2 * H], U8, "w2_raw", "slot_d")
+        w2 = kept([P, 2 * H], U8, "w2")
+        gain_sb = kept([P, 2, 4], F32, "gain_sb")
+        vec_sb = kept([P, 2, 4], F32, "vec_sb")
+        wgt_sb = shared([P, M], F32, "wgt_sb", "slot_f")
+        pages = [kept([P, T2], F32, "page%d" % i) for i in range(PAGES)]
+
+        def load_rows(raw, w, a, c):
+            nc.sync.dma_start(raw, w[K * a : K * (a + 1), BANK * c : BANK * (c + 1)].rearrange("(p j) n -> p j n", j=4))
+
+        def load_w1(b):
+            raw = shared([P, 4, BANK], F32, "w1_raw%d" % b, "slot_b")
+            load_rows(raw[:], w1, 0, b)
+            return raw[:]
+
+        def load_w3(c, tag):
+            raw = shared([P, 2, 4, BANK], F32, "w3_raw%d" % c, tag)
+            for a in range(2):
+                load_rows(raw[:, a], w3, a, c)
+            return raw
+
+        def load_w4(c, tag):
+            raw = shared([P, 2, BANK], I32, "w4_raw%d" % c, tag)
+            nc.sync.dma_start(raw[:], w4_words[:, :, BANK * c : BANK * (c + 1), :].rearrange("a p n i -> p a (n i)").bitcast(I32))
+            return raw
+
+        nc.vector.memset(warm[:, 0:1], 1.0)
+        nc.vector.memset(tab_s[:].bitcast(I32), 0)
+
+        nc.sync.dma_start(list1[:], offs)
+        nc.sync.dma_start(list2[:], offs2)
+        nc.sync.dma_start(list3[:], offs3)
+        nc.sync.dma_start(vec_sb[:], vec.rearrange("(b p i) -> p b i", b=2, i=4))
+        nc.sync.dma_start(gain_sb[:], gain.rearrange("(b p i) -> p b i", b=2, i=4))
+        w1_raw = [load_w1(0)]
+        nc.sync.dma_start(w2_raw[:].bitcast(I32), w2_words[0].bitcast(I32))
+        nc.sync.dma_start(wgt_sb[:], wgt)
+        nc.scalar.activation(warm[:, 1:2], warm[:, 0:1], ACT.Ln)
+        for q in range(4):
+            nc.sync.dma_start(tab_s[32 * q : 32 * q + 4, :].bitcast(I32), tab_scales[0, 4 * q : 4 * q + 4, :].bitcast(I32))
+        tab_w = shared([P, T], I32, "tab_w", "slot_a")
+        nc.sync.dma_start(tab_w[:], tab_words[0].rearrange("p t i -> p (t i)").bitcast(I32))
+
+        for page in pages:
+            nc.vector.memset(page[:], 0.0)
+        nc.vector.memset(s2_raw[:].bitcast(I32), 0)
+        for q in range(4):
+            nc.sync.dma_start(s2_raw[32 * q : 32 * q + 4, :].bitcast(I32), w2_scales[0, 4 * q : 4 * q + 4, :].bitcast(I32))
+
+        v_s = kept([P, S], U8, "v_s")
+
+        def round_columns(copy, raw, t0, nt, dst):
+            copy(
+                dst.rearrange("p (t m j) -> p m j t", t=nt, j=4),
+                raw.rearrange("p j (m t) -> p m j t", t=4)[:, :, :, t0 : t0 + nt],
+            )
+
+        def quantise(rounded, name):
+            codes = kept([P, BANK], U32, name + "_codes")
+            scales = kept([P, BANK], U8, name + "_scales")
+            nc.vector.quantize_mx(out=codes[:].bitcast(FP8X4), scales=scales[:], in_=rounded[:])
+            return codes, scales
+
+        def staged():
+            return ring.tile([P, 4 * BANK], BF16, name="rounded", bufs=3, align_bytes=64)
+
+        w1_rounded = [staged()]
+        round_columns(nc.scalar.copy, w1_raw[0], 0, 4, w1_rounded[0][:])
+        nc.vector.tensor_copy(v_s[:], tab_s[:].indirect(list1[:]))
+        for b in range(2):
+            cols = slice(2 * BANK * b, 2 * BANK * (b + 1))
+            nc.vector.tensor_copy(
+                w2[:, cols].rearrange("p (t m e) -> p t m e", t=4, e=2),
+                w2_raw[:, cols].rearrange("p (m t e) -> p t m e", t=4, e=2),
+            )
+        w1_q = [quantise(w1_rounded[0], "w1_0")]
+
+        def deal_scales(dst, raw):
+            nc.vector.tensor_copy(
+                dst[:].rearrange("p (b t m) -> p b t m", b=2, t=4),
+                raw[:].rearrange("p (b m t) -> p b t m", b=2, t=4),
+            )
+
+        deal_scales(s2, s2_raw)
+        wv = kept([P, 8, M], F32, "wv")
+        for s in range(8):
+            nc.scalar.activation(wv[:, s, :], wgt_sb[:], ACT.Copy, scale=vec_sb[:, s // 4, s % 4 : s % 4 + 1])
+
+        v_w = []
+        for half in range(2):
+            picked = kept([P, BANK], U32, "v_w%d" % half)
+            nc.vector.tensor_copy(picked[:], tab_w[:].bitcast(U32).indirect(list1[:, 32 * half : 32 * (half + 1)]))
+            v_w.append(picked)
+
+        w1_raw.append(load_w1(1))
+        s4_raw = shared([P, H], U8, "s4_raw", "slot_e")
+        nc.vector.memset(s4_raw[:].bitcast(I32), 0)
+        for q in range(4):
+            nc.sync.dma_start(s4_raw[32 * q : 32 * q + 8, :].bitcast(I32), w4_scales[:, 4 * q : 4 * q + 4, :].bitcast(I32))
+        w4_raw = [load_w4(0, "slot_c"), load_w4(1, "slot_d")]
+        w3_raw = [load_w3(0, "slot_a")]
+        wgo_sb = shared([P, M], F32, "wgo_sb", "slot_f")
+        nc.sync.dma_start(wgo_sb[:], wgo)
+        w4 = [kept([P, 2, BANK], I32, "w4_%d" % c) for c in range(2)]
+
+        def deal_w4(c):
+            nc.vector.tensor_copy(
+                w4[c][:].rearrange("p a (t g i) -> p a g t i", t=4, i=4),
+                w4_raw[c][:].rearrange("p a (g i t) -> p a g t i", t=4, i=4),
+            )
+
+        def round_w3(unit):
+            c, pair = divmod(unit, 2)
+            rounded = staged()
+            for a in range(2):
+                round_columns(nc.scalar.copy, w3_raw[c][:, a], 2 * pair, 2, rounded[:, 2 * BANK * a : 2 * BANK * (a + 1)])
+            return rounded
+
+        def interleave(copy, x4, rounded, lo, hi):
+            copy(
+                rounded[:, 4 * lo : 4 * hi].rearrange("p (c i t) -> p c t i", i=4, t=4),
+                x4[:, :, lo:hi].rearrange("p t (c i) -> p c t i", i=4),
+            )
+
+        x4 = [kept([P, 4, M], F32, "x4_%d" % b) for b in range(2)]
+        h_tiles = []
+
+        def stage1_half(s, half):
+            b, t = divmod(s, 4)
+            if half == 0:
+                h_tiles.append(ring.tile([P, S], F32, name="h", bufs=3))
+            cols = slice(BANK * half, BANK * (half + 1))
+            acc_a = psum.tile([P, BANK], F32, name="acc_a", bufs=3)
+            acc_b = psum.tile([P, BANK], F32, name="acc_b", bufs=3)
+            codes, scales = w1_q[b]
+            nc.tensor.matmul_mx(
+                out=acc_a[:], lhsT=codes[:, P * t : P * (t + 1)].bitcast(FP8X4), lhsT_scale=scales[:, P * t : P * (t + 1)],
+                rhs=v_w[half][:].bitcast(FP8X4), rhs_scale=v_s[:, cols], start=True, stop=True,
+            )
+            nc.tensor.matmul_mx(
+                out=acc_b[:], lhsT=w2[:, 2 * P * s : 2 * P * (s + 1)].bitcast(FP4X4), lhsT_scale=s2[:, P * s : P * (s + 1)],
+                rhs=v_w[half][:].bitcast(FP8X4), rhs_scale=v_s[:, cols], start=True, stop=True,
+            )
+            size = ring.tile([P, BANK], F32, name="size", bufs=2)
+            logged = ring.tile([P, BANK], F32, name="logged", bufs=3)
+            nc.scalar.activation(size[:], acc_a[:], ACT.Abs)
+            nc.scalar.activation(logged[:], size[:], ACT.Ln, bias=1.0)
+            nc.vector.scalar_tensor_tensor(h_tiles[s][:, cols], logged[:], gain_sb[:, b, t : t + 1], acc_b[:], ALU.mult, ALU.add)
+
+        def pick(s):
+            nc.vector.tensor_tensor(x4[s // 4][:, s % 4, :], h_tiles[s][:].indirect(list2[:]), wv[:, s, :], ALU.mult)
+
+        z_q = []
+        w3_q = []
+        held = {}
+        for s in range(8):
+            stage1_half(s, 0)
+            if s > 0:
+                pick(s - 1)
+            if s == 1:
+                held["w1"] = staged()
+                round_columns(nc.vector.tensor_copy, w1_raw[1], 0, 4, held["w1"][:])
+                w3_raw.append(load_w3(1, "slot_b"))
+            if s == 2:
+                w1_q.append(quantise(held["w1"], "w1_1"))
+            if s == 4:
+                held["z"] = staged()
+                interleave(nc.scalar.copy, x4[0], held["z"], 0, M)
+            if s == 3:
+                deal_scales(s4, s4_raw)
+            if s == 5:
+                deal_w4(0)
+            if s == 6:
+                z_q.append(quantise(held["z"], "z_0"))
+            stage1_half(s, 1)
+        held["w3"] = round_w3(0)
+        pick(7)
+        w3_q.append(quantise(held["w3"], "w3_0"))
+        held["z"] = staged()
+        interleave(nc.vector.tensor_copy, x4[1], held["z"], 0, M)
+        z_q.append(quantise(held["z"], "z_1"))
+        deal_w4(1)
+
+        larger = []
+
+        def stage2(s):
+            c, t = divmod(s, 4)
+            acc_1 = psum.tile([P, BANK], F32, name="acc_1", bufs=1)
+            acc_2 = psum.tile([P, BANK], F32, name="acc_2", bufs=1)
+            codes, scales = w3_q[s // 2]
+            for a in range(2):
+                cols = slice(P * (2 * a + s % 2), P * (2 * a + s % 2 + 1))
+                nc.tensor.matmul_mx(
+                    out=acc_1[:], lhsT=codes[:, cols].bitcast(FP8X4), lhsT_scale=scales[:, cols],
+                    rhs=z_q[a][0][:].bitcast(FP8X4), rhs_scale=z_q[a][1][:], start=(a == 0), stop=(a == 1),
+                )
+            for a in range(2):
+                nc.tensor.matmul_mx(
+                    out=acc_2[:], lhsT=w4[c][:, a, P * t : P * (t + 1)].bitcast(FP8X4),
+                    lhsT_scale=s4[4 * a : P, P * s : P * (s + 1)],
+                    rhs=z_q[a][0][:].bitcast(FP8X4), rhs_scale=z_q[a][1][:], start=(a == 0), stop=(a == 1),
+                )
+            size_1 = ring.tile([P, M], F32, name="size_1", bufs=2)
+            size_2 = ring.tile([P, M], F32, name="size_2", bufs=2)
+            nc.scalar.activation(size_1[:], acc_1[:], ACT.Abs)
+            nc.scalar.activation(size_2[:], acc_2[:], ACT.Abs)
+            y = ring.tile([P, M], F32, name="y", bufs=3)
+            nc.vector.tensor_tensor(y[:], size_1[:], size_2[:], ALU.max)
+            larger.append(y)
+
+        def file_rows(s):
+            c, t = divmod(s, 4)
+            page = pages[s % PAGES]
+            nc.vector.tensor_tensor(page[:].indirect(list3[:]), larger[s][:], wgo_sb[:], ALU.mult)
+            nc.sync.dma_start(out[BANK * c : BANK * (c + 1), :].rearrange("(p i) s -> p i s", i=4)[:, t, :], page[:])
+
+        for s in range(8):
+            stage2(s)
+            if s % 2 == 0 and s < 6:
+                held["w3"] = round_w3(s // 2 + 1)
+            if s > 0:
+                file_rows(s - 1)
+            if s % 2 == 1 and s < 6:
+                w3_q.append(quantise(held["w3"], "w3_%d" % (s // 2 + 1)))
+        file_rows(7)

@@ -41,8 +41,6 @@ def tile_list_inflator_severity_filing_kernel(
         list3 = kept([P, M // 16], U16, "list3")
         tab_s = shared([P, T], U8, "tab_s", "slot_c")
         s2_raw = shared([P, H], U8, "s2_raw", "slot_e")
-        s2 = kept([P, H], U8, "s2")
-        s4 = kept([P, H], U8, "s4")
         warm = shared([P, 2], F32, "warm", "slot_a")
         w2_raw = shared([P, 2 * H], U8, "w2_raw", "slot_d")
         w2 = kept([P, 2 * H], U8, "w2")
@@ -73,11 +71,14 @@ def tile_list_inflator_severity_filing_kernel(
         nc.vector.memset(warm[:, 0:1], 1.0)
         nc.vector.memset(tab_s[:].bitcast(I32), 0)
 
+        for q in range(4):
+            rows = w2_scales[0, 4 * q : 4 * q + 4, :].bitcast(I32)
+            nc.sync.dma_start(s2_raw[32 * q : 32 * (q + 1), :].bitcast(I32), rows.partition_broadcast(8))
         nc.sync.dma_start(list1[:], offs)
         nc.sync.dma_start(list2[:], offs2)
         nc.sync.dma_start(list3[:], offs3)
-        nc.sync.dma_start(vec_sb[:], vec.rearrange("(b p i) -> p b i", b=2, i=4))
-        nc.sync.dma_start(gain_sb[:], gain.rearrange("(b p i) -> p b i", b=2, i=4))
+        nc.gpsimd.dma_start(vec_sb[:], vec.rearrange("(b p i) -> p b i", b=2, i=4))
+        nc.gpsimd.dma_start(gain_sb[:], gain.rearrange("(b p i) -> p b i", b=2, i=4))
         w1_raw = [load_w1(0)]
         nc.sync.dma_start(w2_raw[:].bitcast(I32), w2_words[0].bitcast(I32))
         nc.sync.dma_start(wgt_sb[:], wgt)
@@ -89,9 +90,6 @@ def tile_list_inflator_severity_filing_kernel(
 
         for page in pages:
             nc.vector.memset(page[:], 0.0)
-        nc.vector.memset(s2_raw[:].bitcast(I32), 0)
-        for q in range(4):
-            nc.sync.dma_start(s2_raw[32 * q : 32 * q + 4, :].bitcast(I32), w2_scales[0, 4 * q : 4 * q + 4, :].bitcast(I32))
 
         v_s = kept([P, S], U8, "v_s")
 
@@ -100,6 +98,10 @@ def tile_list_inflator_severity_filing_kernel(
                 dst.rearrange("p (t m j) -> p m j t", t=nt, j=4),
                 raw.rearrange("p j (m t) -> p m j t", t=4)[:, :, :, t0 : t0 + nt],
             )
+
+        def round_half(copy, raw, rounded):
+            for pair in range(2):
+                round_columns(copy[pair], raw, 2 * pair, 2, rounded[:, 2 * BANK * pair : 2 * BANK * (pair + 1)])
 
         def quantise(rounded, name):
             codes = kept([P, BANK], U32, name + "_codes")
@@ -111,7 +113,7 @@ def tile_list_inflator_severity_filing_kernel(
             return ring.tile([P, 4 * BANK], BF16, name="rounded", bufs=3, align_bytes=64)
 
         w1_rounded = [staged()]
-        round_columns(nc.scalar.copy, w1_raw[0], 0, 4, w1_rounded[0][:])
+        round_half((nc.vector.tensor_copy, nc.scalar.copy), w1_raw[0], w1_rounded[0])
         nc.vector.tensor_copy(v_s[:], tab_s[:].indirect(list1[:]))
         for b in range(2):
             cols = slice(2 * BANK * b, 2 * BANK * (b + 1))
@@ -123,11 +125,12 @@ def tile_list_inflator_severity_filing_kernel(
 
         def deal_scales(dst, raw):
             nc.vector.tensor_copy(
-                dst[:].rearrange("p (b t m) -> p b t m", b=2, t=4),
-                raw[:].rearrange("p (b m t) -> p b t m", b=2, t=4),
+                dst.rearrange("p (b t m) -> p b t m", t=4, m=P),
+                raw.rearrange("p (b m t) -> p b t m", t=4, m=P),
             )
 
-        deal_scales(s2, s2_raw)
+        s2 = kept([P, H], U8, "s2")
+        deal_scales(s2[:], s2_raw[:])
         wv = kept([P, 8, M], F32, "wv")
         for s in range(8):
             nc.scalar.activation(wv[:, s, :], wgt_sb[:], ACT.Copy, scale=vec_sb[:, s // 4, s % 4 : s % 4 + 1])
@@ -139,17 +142,14 @@ def tile_list_inflator_severity_filing_kernel(
             v_w.append(picked)
 
         w1_raw.append(load_w1(1))
-        s4_raw = shared([P, H], U8, "s4_raw", "slot_e")
-        nc.vector.memset(s4_raw[:].bitcast(I32), 0)
-        for q in range(4):
-            nc.sync.dma_start(s4_raw[32 * q : 32 * q + 8, :].bitcast(I32), w4_scales[:, 4 * q : 4 * q + 4, :].bitcast(I32))
         w4_raw = [load_w4(0, "slot_c"), load_w4(1, "slot_d")]
         w3_raw = [load_w3(0, "slot_a")]
         wgo_sb = shared([P, M], F32, "wgo_sb", "slot_f")
         nc.sync.dma_start(wgo_sb[:], wgo)
-        w4 = [kept([P, 2, BANK], I32, "w4_%d" % c) for c in range(2)]
+        w4 = []
 
-        def deal_w4(c):
+        def deal_w4(c, tag):
+            w4.append(shared([P, 2, BANK], I32, "w4_%d" % c, tag))
             nc.vector.tensor_copy(
                 w4[c][:].rearrange("p a (t g i) -> p a g t i", t=4, i=4),
                 w4_raw[c][:].rearrange("p a (g i t) -> p a g t i", t=4, i=4),
@@ -168,30 +168,47 @@ def tile_list_inflator_severity_filing_kernel(
                 x4[:, :, lo:hi].rearrange("p t (c i) -> p c t i", i=4),
             )
 
-        x4 = [kept([P, 4, M], F32, "x4_%d" % b) for b in range(2)]
+        x4 = [shared([P, 4, M], F32, "x4_%d" % b, "x4_%d" % b) for b in range(2)]
+        first_tenant = {0: "s4_raw", 1: "s4_raw", 7: "s4", 9: "w4_0"}
         h_tiles = []
+        sizes = []
 
-        def stage1_half(s, half):
+        def stage1_products(i):
+            s, half = divmod(i, 2)
             b, t = divmod(s, 4)
-            if half == 0:
-                h_tiles.append(ring.tile([P, S], F32, name="h", bufs=3))
             cols = slice(BANK * half, BANK * (half + 1))
-            acc_a = psum.tile([P, BANK], F32, name="acc_a", bufs=3)
-            acc_b = psum.tile([P, BANK], F32, name="acc_b", bufs=3)
+            acc_a = psum.tile([P, BANK], F32, name="acc_a", bufs=2)
             codes, scales = w1_q[b]
             nc.tensor.matmul_mx(
                 out=acc_a[:], lhsT=codes[:, P * t : P * (t + 1)].bitcast(FP8X4), lhsT_scale=scales[:, P * t : P * (t + 1)],
                 rhs=v_w[half][:].bitcast(FP8X4), rhs_scale=v_s[:, cols], start=True, stop=True,
             )
+            if half == 0 and s > 0:
+                size = x4[(s - 1) // 4][:, (s - 1) % 4, :]
+            elif i in first_tenant:
+                size = shared([P, BANK], F32, "size_%d" % i, first_tenant[i])[:]
+            else:
+                size_tile = ring.tile([P, BANK], F32, name="size", bufs=2)
+                size = size_tile[:]
+            nc.scalar.activation(size, acc_a[:], ACT.Abs)
+            sizes.append(size)
+
+        def stage1_join(i):
+            s, half = divmod(i, 2)
+            b, t = divmod(s, 4)
+            if half == 0:
+                h_tiles.append(ring.tile([P, S], F32, name="h", bufs=3))
+            cols = slice(BANK * half, BANK * (half + 1))
+            acc_b = psum.tile([P, BANK], F32, name="acc_b", bufs=4)
             nc.tensor.matmul_mx(
                 out=acc_b[:], lhsT=w2[:, 2 * P * s : 2 * P * (s + 1)].bitcast(FP4X4), lhsT_scale=s2[:, P * s : P * (s + 1)],
                 rhs=v_w[half][:].bitcast(FP8X4), rhs_scale=v_s[:, cols], start=True, stop=True,
             )
-            size = ring.tile([P, BANK], F32, name="size", bufs=2)
             logged = ring.tile([P, BANK], F32, name="logged", bufs=3)
-            nc.scalar.activation(size[:], acc_a[:], ACT.Abs)
-            nc.scalar.activation(logged[:], size[:], ACT.Ln, bias=1.0)
-            nc.vector.scalar_tensor_tensor(h_tiles[s][:, cols], logged[:], gain_sb[:, b, t : t + 1], acc_b[:], ALU.mult, ALU.add)
+            nc.scalar.activation(logged[:], sizes[i], ACT.Ln, bias=1.0)
+            nc.vector.scalar_tensor_tensor(
+                h_tiles[s][:, cols], logged[:], gain_sb[:, b, t : t + 1], acc_b[:], ALU.mult, ALU.add
+            )
 
         def pick(s):
             nc.vector.tensor_tensor(x4[s // 4][:, s % 4, :], h_tiles[s][:].indirect(list2[:]), wv[:, s, :], ALU.mult)
@@ -199,73 +216,92 @@ def tile_list_inflator_severity_filing_kernel(
         z_q = []
         w3_q = []
         held = {}
-        for s in range(8):
-            stage1_half(s, 0)
-            if s > 0:
-                pick(s - 1)
-            if s == 1:
+        stage1_products(0)
+        for i in range(16):
+            if 0 < i < 15:
+                stage1_products(i + 1)
+            stage1_join(i)
+            if i == 0:
+                stage1_products(1)
+            if i % 2 == 0 and i > 0:
+                pick(i // 2 - 1)
+            if i == 1:
+                s4_raw = shared([P, H], U8, "s4_raw", "s4_raw")
+                nc.vector.memset(s4_raw[:].bitcast(I32), 0)
+                for q in range(4):
+                    nc.sync.dma_start(s4_raw[32 * q : 32 * q + 8, :].bitcast(I32), w4_scales[:, 4 * q : 4 * q + 4, :].bitcast(I32))
+            if i == 0:
                 held["w1"] = staged()
-                round_columns(nc.vector.tensor_copy, w1_raw[1], 0, 4, held["w1"][:])
+                round_half((nc.vector.tensor_copy, nc.vector.tensor_copy), w1_raw[1], held["w1"])
                 w3_raw.append(load_w3(1, "slot_b"))
-            if s == 2:
+            if i == 1:
                 w1_q.append(quantise(held["w1"], "w1_1"))
-            if s == 4:
+            if i == 7:
+                s4 = shared([P, H], U8, "s4", "s4")
+                deal_scales(s4[:], s4_raw[:])
+            if i == 8:
                 held["z"] = staged()
                 interleave(nc.scalar.copy, x4[0], held["z"], 0, M)
-            if s == 3:
-                deal_scales(s4, s4_raw)
-            if s == 5:
-                deal_w4(0)
-            if s == 6:
+            if i == 9:
+                deal_w4(0, "w4_0")
+            if i == 12:
                 z_q.append(quantise(held["z"], "z_0"))
-            stage1_half(s, 1)
         held["w3"] = round_w3(0)
         pick(7)
         w3_q.append(quantise(held["w3"], "w3_0"))
-        held["z"] = staged()
-        interleave(nc.vector.tensor_copy, x4[1], held["z"], 0, M)
-        z_q.append(quantise(held["z"], "z_1"))
-        deal_w4(1)
+        z_last = staged()
+        z_codes = kept([P, M], U32, "z_1_codes")
+        z_scales = kept([P, M], U8, "z_1_scales")
+        z_q.append((z_codes, z_scales))
+        interleave(nc.vector.tensor_copy, x4[1], z_last, 0, M // 2)
+        interleave(nc.scalar.copy, x4[1], z_last, M // 2, M)
+        for lo in (0, M // 2):
+            cols = slice(lo, lo + M // 2)
+            nc.vector.quantize_mx(out=z_codes[:, cols].bitcast(FP8X4), scales=z_scales[:, cols], in_=z_last[:, 4 * lo : 4 * lo + 2 * M])
+        deal_w4(1, "x4_1")
 
-        larger = []
-
-        def stage2(s):
+        def stage2(s, lo, hi, tags, size_1, size_2):
             c, t = divmod(s, 4)
-            acc_1 = psum.tile([P, BANK], F32, name="acc_1", bufs=1)
-            acc_2 = psum.tile([P, BANK], F32, name="acc_2", bufs=1)
+            acc_1 = psum.tile([P, BANK], F32, name="acc_1", tag=tags[0], bufs=tags[2])
+            acc_2 = psum.tile([P, BANK], F32, name="acc_2", tag=tags[1], bufs=tags[2])
             codes, scales = w3_q[s // 2]
             for a in range(2):
                 cols = slice(P * (2 * a + s % 2), P * (2 * a + s % 2 + 1))
                 nc.tensor.matmul_mx(
-                    out=acc_1[:], lhsT=codes[:, cols].bitcast(FP8X4), lhsT_scale=scales[:, cols],
-                    rhs=z_q[a][0][:].bitcast(FP8X4), rhs_scale=z_q[a][1][:], start=(a == 0), stop=(a == 1),
+                    out=acc_1[:, 0 : hi - lo], lhsT=codes[:, cols].bitcast(FP8X4), lhsT_scale=scales[:, cols],
+                    rhs=z_q[a][0][:, lo:hi].bitcast(FP8X4), rhs_scale=z_q[a][1][:, lo:hi], start=(a == 0), stop=(a == 1),
                 )
             for a in range(2):
                 nc.tensor.matmul_mx(
-                    out=acc_2[:], lhsT=w4[c][:, a, P * t : P * (t + 1)].bitcast(FP8X4),
+                    out=acc_2[:, 0 : hi - lo], lhsT=w4[c][:, a, P * t : P * (t + 1)].bitcast(FP8X4),
                     lhsT_scale=s4[4 * a : P, P * s : P * (s + 1)],
-                    rhs=z_q[a][0][:].bitcast(FP8X4), rhs_scale=z_q[a][1][:], start=(a == 0), stop=(a == 1),
+                    rhs=z_q[a][0][:, lo:hi].bitcast(FP8X4), rhs_scale=z_q[a][1][:, lo:hi], start=(a == 0), stop=(a == 1),
                 )
-            size_1 = ring.tile([P, M], F32, name="size_1", bufs=2)
-            size_2 = ring.tile([P, M], F32, name="size_2", bufs=2)
-            nc.scalar.activation(size_1[:], acc_1[:], ACT.Abs)
-            nc.scalar.activation(size_2[:], acc_2[:], ACT.Abs)
-            y = ring.tile([P, M], F32, name="y", bufs=3)
-            nc.vector.tensor_tensor(y[:], size_1[:], size_2[:], ALU.max)
-            larger.append(y)
+            nc.scalar.activation(size_1, acc_1[:, 0 : hi - lo], ACT.Abs)
+            nc.scalar.activation(size_2, acc_2[:, 0 : hi - lo], ACT.Abs)
 
-        def file_rows(s):
-            c, t = divmod(s, 4)
-            page = pages[s % PAGES]
-            nc.vector.tensor_tensor(page[:].indirect(list3[:]), larger[s][:], wgo_sb[:], ALU.mult)
-            nc.sync.dma_start(out[BANK * c : BANK * (c + 1), :].rearrange("(p i) s -> p i s", i=4)[:, t, :], page[:])
+        def larger(parts):
+            size_1 = ring.tile([P, 2 * M], F32, name="size_1", bufs=2)
+            size_2 = ring.tile([P, 2 * M], F32, name="size_2", bufs=2)
+            y = ring.tile([P, 2 * M], F32, name="y", bufs=2)
+            at = 0
+            for s, lo, hi, tags in parts:
+                stage2(s, lo, hi, tags, size_1[:, at : at + hi - lo], size_2[:, at : at + hi - lo])
+                at = at + hi - lo
+            nc.vector.tensor_tensor(y[:, 0:at], size_1[:, 0:at], size_2[:, 0:at], ALU.max)
+            at = 0
+            for s, lo, hi, tags in parts:
+                page = pages[s % PAGES]
+                nc.vector.tensor_tensor(page[:].indirect(list3[:, lo // 16 : hi // 16]), y[:, at : at + hi - lo], wgo_sb[:, lo:hi], ALU.mult)
+                at = at + hi - lo
+                if hi == M:
+                    c, t = divmod(s, 4)
+                    nc.sync.dma_start(out[BANK * c : BANK * (c + 1), :].rearrange("(p i) s -> p i s", i=4)[:, t, :], page[:])
 
-        for s in range(8):
-            stage2(s)
-            if s % 2 == 0 and s < 6:
-                held["w3"] = round_w3(s // 2 + 1)
-            if s > 0:
-                file_rows(s - 1)
-            if s % 2 == 1 and s < 6:
-                w3_q.append(quantise(held["w3"], "w3_%d" % (s // 2 + 1)))
-        file_rows(7)
+        own = ("acc_1", "acc_2", 1)
+        larger([(0, 0, M // 2, own)])
+        larger([(0, M // 2, M, ("acc_a", "acc_a", 2))])
+        for group in ([1], [2, 3], [4, 5], [6, 7]):
+            if len(w3_q) < 4:
+                w3_q.append(quantise(round_w3(len(w3_q)), "w3_%d" % len(w3_q)))
+            larger([(s, 0, M, own) for s in group])

from contextlib import ExitStack

import concourse.mybir as mybir

K, T, S, H, N, M, T2 = 512, 4096, 1024, 1024, 1024, 512, 1024
FLOPS = 2 * (2 * K * H * S + 2 * H * N * M)

F32 = mybir.dt.float32
BF16 = mybir.dt.bfloat16
I32 = mybir.dt.int32
U32 = mybir.dt.uint32
U16 = mybir.dt.uint16
U8 = mybir.dt.uint8
FP8X4 = mybir.dt.float8_e4m3fn_x4
FP4X4 = mybir.dt.float4_e2m1fn_x4
ALU = mybir.AluOpType
ACT = mybir.ActivationFunctionType

P = 128
BANK = 512
PAGES = 3


def tile_list_inflator_severity_filing_kernel(
    tc, tab_words, tab_scales, offs, w1, w2_words, w2_scales, gain, offs2, wgt, vec, w3, w4_words, w4_scales, offs3, wgo, out
):
    nc = tc.nc
    with ExitStack() as ctx:
        keep = ctx.enter_context(tc.tile_pool(name="keep", bufs=1))
        ring = ctx.enter_context(tc.tile_pool(name="ring", bufs=2))
        psum = ctx.enter_context(tc.psum_pool(name="psum", bufs=1))

        def kept(shape, dtype, name):
            return keep.tile(shape, dtype, name=name, align_bytes=64)

        def shared(shape, dtype, name, tag):
            return keep.tile(shape, dtype, name=name, tag=tag, align_bytes=64)

        list1 = kept([P, S // 16], U16, "list1")
        list2 = kept([P, M // 16], U16, "list2")
        list3 = kept([P, M // 16], U16, "list3")
        tab_s = shared([P, T], U8, "tab_s", "slot_c")
        s2_raw = shared([P, H], U8, "s2_raw", "slot_e")
        warm = shared([P, 2], F32, "warm", "slot_a")
        w2_raw = shared([P, 2 * H], U8, "w2_raw", "slot_d")
        w2 = kept([P, 2 * H], U8, "w2")
        gain_sb = kept([P, 2, 4], F32, "gain_sb")
        vec_sb = kept([P, 2, 4], F32, "vec_sb")
        wgt_sb = shared([P, M], F32, "wgt_sb", "slot_f")
        pages = [kept([P, T2], F32, "page%d" % i) for i in range(PAGES)]

        def load_rows(raw, w, a, c):
            nc.sync.dma_start(raw, w[K * a : K * (a + 1), BANK * c : BANK * (c + 1)].rearrange("(p j) n -> p j n", j=4))

        def load_w1(b):
            raw = shared([P, 4, BANK], F32, "w1_raw%d" % b, "slot_b")
            load_rows(raw[:], w1, 0, b)
            return raw[:]

        def load_w3(c, tag):
            raw = shared([P, 2, 4, BANK], F32, "w3_raw%d" % c, tag)
            for a in range(2):
                load_rows(raw[:, a], w3, a, c)
            return raw

        def load_w4(c, tag):
            raw = shared([P, 2, BANK], I32, "w4_raw%d" % c, tag)
            nc.sync.dma_start(raw[:], w4_words[:, :, BANK * c : BANK * (c + 1), :].rearrange("a p n i -> p a (n i)").bitcast(I32))
            return raw

        nc.vector.memset(warm[:, 0:1], 1.0)
        nc.vector.memset(tab_s[:].bitcast(I32), 0)

        for q in range(4):
            rows = w2_scales[0, 4 * q : 4 * q + 4, :].bitcast(I32)
            nc.sync.dma_start(s2_raw[32 * q : 32 * (q + 1), :].bitcast(I32), rows.partition_broadcast(8))
        nc.sync.dma_start(list1[:], offs)
        nc.sync.dma_start(list2[:], offs2)
        nc.sync.dma_start(list3[:], offs3)
        nc.gpsimd.dma_start(vec_sb[:], vec.rearrange("(b p i) -> p b i", b=2, i=4))
        nc.gpsimd.dma_start(gain_sb[:], gain.rearrange("(b p i) -> p b i", b=2, i=4))
        w1_raw = [load_w1(0)]
        nc.sync.dma_start(w2_raw[:].bitcast(I32), w2_words[0].bitcast(I32))
        nc.sync.dma_start(wgt_sb[:], wgt)
        nc.scalar.activation(warm[:, 1:2], warm[:, 0:1], ACT.Ln)
        for q in range(4):
            nc.sync.dma_start(tab_s[32 * q : 32 * q + 4, :].bitcast(I32), tab_scales[0, 4 * q : 4 * q + 4, :].bitcast(I32))
        tab_w = shared([P, T], I32, "tab_w", "slot_a")
        nc.sync.dma_start(tab_w[:], tab_words[0].rearrange("p t i -> p (t i)").bitcast(I32))

        for page in pages:
            nc.vector.memset(page[:], 0.0)

        v_s = kept([P, S], U8, "v_s")

        def round_columns(copy, raw, t0, nt, dst):
            copy(
                dst.rearrange("p (t m j) -> p m j t", t=nt, j=4),
                raw.rearrange("p j (m t) -> p m j t", t=4)[:, :, :, t0 : t0 + nt],
            )

        def round_half(copy, raw, rounded):
            for pair in range(2):
                round_columns(copy[pair], raw, 2 * pair, 2, rounded[:, 2 * BANK * pair : 2 * BANK * (pair + 1)])

        def quantise(rounded, name):
            codes = kept([P, BANK], U32, name + "_codes")
            scales = kept([P, BANK], U8, name + "_scales")
            nc.vector.quantize_mx(out=codes[:].bitcast(FP8X4), scales=scales[:], in_=rounded[:])
            return codes, scales

        def staged():
            return ring.tile([P, 4 * BANK], BF16, name="rounded", bufs=3, align_bytes=64)

        w1_rounded = [staged()]
        round_half((nc.vector.tensor_copy, nc.scalar.copy), w1_raw[0], w1_rounded[0])
        nc.vector.tensor_copy(v_s[:], tab_s[:].indirect(list1[:]))
        for b in range(2):
            cols = slice(2 * BANK * b, 2 * BANK * (b + 1))
            nc.vector.tensor_copy(
                w2[:, cols].rearrange("p (t m e) -> p t m e", t=4, e=2),
                w2_raw[:, cols].rearrange("p (m t e) -> p t m e", t=4, e=2),
            )
        w1_q = [quantise(w1_rounded[0], "w1_0")]

        def deal_scales(dst, raw):
            nc.vector.tensor_copy(
                dst.rearrange("p (b t m) -> p b t m", t=4, m=P),
                raw.rearrange("p (b m t) -> p b t m", t=4, m=P),
            )

        s2 = kept([P, H], U8, "s2")
        deal_scales(s2[:], s2_raw[:])
        wv = kept([P, 8, M], F32, "wv")
        for s in range(8):
            nc.scalar.activation(wv[:, s, :], wgt_sb[:], ACT.Copy, scale=vec_sb[:, s // 4, s % 4 : s % 4 + 1])

        v_w = []
        for half in range(2):
            picked = kept([P, BANK], U32, "v_w%d" % half)
            nc.vector.tensor_copy(picked[:], tab_w[:].bitcast(U32).indirect(list1[:, 32 * half : 32 * (half + 1)]))
            v_w.append(picked)

        w1_raw.append(load_w1(1))
        w4_raw = [load_w4(0, "slot_c"), load_w4(1, "slot_d")]
        w3_raw = [load_w3(0, "slot_a")]
        wgo_sb = shared([P, M], F32, "wgo_sb", "slot_f")
        nc.sync.dma_start(wgo_sb[:], wgo)
        w4 = []

        def deal_w4(c, tag):
            w4.append(shared([P, 2, BANK], I32, "w4_%d" % c, tag))
            nc.vector.tensor_copy(
                w4[c][:].rearrange("p a (t g i) -> p a g t i", t=4, i=4),
                w4_raw[c][:].rearrange("p a (g i t) -> p a g t i", t=4, i=4),
            )

        def round_w3(unit):
            c, pair = divmod(unit, 2)
            rounded = staged()
            for a in range(2):
                round_columns(nc.scalar.copy, w3_raw[c][:, a], 2 * pair, 2, rounded[:, 2 * BANK * a : 2 * BANK * (a + 1)])
            return rounded

        def interleave(copy, x4, rounded, lo, hi):
            copy(
                rounded[:, 4 * lo : 4 * hi].rearrange("p (c i t) -> p c t i", i=4, t=4),
                x4[:, :, lo:hi].rearrange("p t (c i) -> p c t i", i=4),
            )

        x4 = [shared([P, 4, M], F32, "x4_%d" % b, "x4_%d" % b) for b in range(2)]
        first_tenant = {0: "s4_raw", 1: "s4_raw", 7: "s4", 9: "w4_0"}
        h_tiles = []
        sizes = []

        def stage1_products(i):
            s, half = divmod(i, 2)
            b, t = divmod(s, 4)
            cols = slice(BANK * half, BANK * (half + 1))
            acc_a = psum.tile([P, BANK], F32, name="acc_a", bufs=2)
            codes, scales = w1_q[b]
            nc.tensor.matmul_mx(
                out=acc_a[:], lhsT=codes[:, P * t : P * (t + 1)].bitcast(FP8X4), lhsT_scale=scales[:, P * t : P * (t + 1)],
                rhs=v_w[half][:].bitcast(FP8X4), rhs_scale=v_s[:, cols], start=True, stop=True,
            )
            if half == 0 and s > 0:
                size = x4[(s - 1) // 4][:, (s - 1) % 4, :]
            elif i in first_tenant:
                size = shared([P, BANK], F32, "size_%d" % i, first_tenant[i])[:]
            else:
                size_tile = ring.tile([P, BANK], F32, name="size", bufs=2)
                size = size_tile[:]
            nc.scalar.activation(size, acc_a[:], ACT.Abs)
            sizes.append(size)

        def stage1_join(i):
            s, half = divmod(i, 2)
            b, t = divmod(s, 4)
            if half == 0:
                h_tiles.append(ring.tile([P, S], F32, name="h", bufs=3))
            cols = slice(BANK * half, BANK * (half + 1))
            acc_b = psum.tile([P, BANK], F32, name="acc_b", bufs=4)
            nc.tensor.matmul_mx(
                out=acc_b[:], lhsT=w2[:, 2 * P * s : 2 * P * (s + 1)].bitcast(FP4X4), lhsT_scale=s2[:, P * s : P * (s + 1)],
                rhs=v_w[half][:].bitcast(FP8X4), rhs_scale=v_s[:, cols], start=True, stop=True,
            )
            logged = ring.tile([P, BANK], F32, name="logged", bufs=3)
            nc.scalar.activation(logged[:], sizes[i], ACT.Ln, bias=1.0)
            nc.vector.scalar_tensor_tensor(
                h_tiles[s][:, cols], logged[:], gain_sb[:, b, t : t + 1], acc_b[:], ALU.mult, ALU.add
            )

        def pick(s):
            nc.vector.tensor_tensor(x4[s // 4][:, s % 4, :], h_tiles[s][:].indirect(list2[:]), wv[:, s, :], ALU.mult)

        z_q = []
        w3_q = []
        held = {}
        stage1_products(0)
        for i in range(16):
            if 0 < i < 15:
                stage1_products(i + 1)
            stage1_join(i)
            if i == 0:
                stage1_products(1)
            if i % 2 == 0 and i > 0:
                pick(i // 2 - 1)
            if i == 1:
                s4_raw = shared([P, H], U8, "s4_raw", "s4_raw")
                nc.vector.memset(s4_raw[:].bitcast(I32), 0)
                for q in range(4):
                    nc.sync.dma_start(s4_raw[32 * q : 32 * q + 8, :].bitcast(I32), w4_scales[:, 4 * q : 4 * q + 4, :].bitcast(I32))
            if i == 0:
                held["w1"] = staged()
                round_half((nc.vector.tensor_copy, nc.vector.tensor_copy), w1_raw[1], held["w1"])
                w3_raw.append(load_w3(1, "slot_b"))
            if i == 1:
                w1_q.append(quantise(held["w1"], "w1_1"))
            if i == 7:
                s4 = shared([P, H], U8, "s4", "s4")
                deal_scales(s4[:], s4_raw[:])
            if i == 8:
                held["z"] = staged()
                interleave(nc.scalar.copy, x4[0], held["z"], 0, M)
            if i == 9:
                deal_w4(0, "w4_0")
            if i == 12:
                z_q.append(quantise(held["z"], "z_0"))
        held["w3"] = round_w3(0)
        pick(7)
        w3_q.append(quantise(held["w3"], "w3_0"))
        z_last = staged()
        z_codes = kept([P, M], U32, "z_1_codes")
        z_scales = kept([P, M], U8, "z_1_scales")
        z_q.append((z_codes, z_scales))
        interleave(nc.vector.tensor_copy, x4[1], z_last, 0, M // 2)
        interleave(nc.scalar.copy, x4[1], z_last, M // 2, M)
        for lo in (0, M // 2):
            cols = slice(lo, lo + M // 2)
            nc.vector.quantize_mx(out=z_codes[:, cols].bitcast(FP8X4), scales=z_scales[:, cols], in_=z_last[:, 4 * lo : 4 * lo + 2 * M])
        deal_w4(1, "x4_1")

        def stage2(s, lo, hi, tags, size_1, size_2):
            c, t = divmod(s, 4)
            acc_1 = psum.tile([P, BANK], F32, name="acc_1", tag=tags[0], bufs=tags[2])
            acc_2 = psum.tile([P, BANK], F32, name="acc_2", tag=tags[1], bufs=tags[2])
            codes, scales = w3_q[s // 2]
            for a in range(2):
                cols = slice(P * (2 * a + s % 2), P * (2 * a + s % 2 + 1))
                nc.tensor.matmul_mx(
                    out=acc_1[:, 0 : hi - lo], lhsT=codes[:, cols].bitcast(FP8X4), lhsT_scale=scales[:, cols],
                    rhs=z_q[a][0][:, lo:hi].bitcast(FP8X4), rhs_scale=z_q[a][1][:, lo:hi], start=(a == 0), stop=(a == 1),
                )
            for a in range(2):
                nc.tensor.matmul_mx(
                    out=acc_2[:, 0 : hi - lo], lhsT=w4[c][:, a, P * t : P * (t + 1)].bitcast(FP8X4),
                    lhsT_scale=s4[4 * a : P, P * s : P * (s + 1)],
                    rhs=z_q[a][0][:, lo:hi].bitcast(FP8X4), rhs_scale=z_q[a][1][:, lo:hi], start=(a == 0), stop=(a == 1),
                )
            nc.scalar.activation(size_1, acc_1[:, 0 : hi - lo], ACT.Abs)
            nc.scalar.activation(size_2, acc_2[:, 0 : hi - lo], ACT.Abs)

        def larger(parts):
            size_1 = ring.tile([P, 2 * M], F32, name="size_1", bufs=2)
            size_2 = ring.tile([P, 2 * M], F32, name="size_2", bufs=2)
            y = ring.tile([P, 2 * M], F32, name="y", bufs=2)
            at = 0
            for s, lo, hi, tags in parts:
                stage2(s, lo, hi, tags, size_1[:, at : at + hi - lo], size_2[:, at : at + hi - lo])
                at = at + hi - lo
            nc.vector.tensor_tensor(y[:, 0:at], size_1[:, 0:at], size_2[:, 0:at], ALU.max)
            at = 0
            for s, lo, hi, tags in parts:
                page = pages[s % PAGES]
                nc.vector.tensor_tensor(page[:].indirect(list3[:, lo // 16 : hi // 16]), y[:, at : at + hi - lo], wgo_sb[:, lo:hi], ALU.mult)
                at = at + hi - lo
                if hi == M:
                    c, t = divmod(s, 4)
                    nc.sync.dma_start(out[BANK * c : BANK * (c + 1), :].rearrange("(p i) s -> p i s", i=4)[:, t, :], page[:])

        own = ("acc_1", "acc_2", 1)
        larger([(0, 0, M // 2, own)])
        larger([(0, M // 2, M, ("acc_a", "acc_a", 2))])
        for group in ([1], [2, 3], [4, 5], [6, 7]):
            if len(w3_q) < 4:
                w3_q.append(quantise(round_w3(len(w3_q)), "w3_%d" % len(w3_q)))
            larger([(s, 0, M, own) for s in group])
